import numpy as np
import ml_dtypes


def mxq(x, axis, fmt="e4m3"):
    dtype, down = {"e4m3": (ml_dtypes.float8_e4m3fn, 7), "e5m2": (ml_dtypes.float8_e5m2, 14)}[fmt]
    v = np.moveaxis(np.asarray(x, np.float32).astype(ml_dtypes.bfloat16).astype(np.float64), axis, -1)
    blocks = v.reshape(v.shape[:-1] + (-1, 32))
    amax = np.abs(blocks).max(-1, keepdims=True)
    byte = np.maximum(np.where(amax > 0, np.frexp(amax)[1] - 1 + 127, 0) - down, 1)
    scale = np.exp2(byte - 127.0)
    codes = (blocks / scale).astype(np.float32).astype(dtype).astype(np.float64)
    return np.moveaxis((codes * scale).reshape(v.shape), -1, axis)


WIDE = False


def mx_kscale(k):
    if not WIDE:
        return np.ones(k)
    levels = np.array([10, -10, 5, -5, 0])
    if k % 512:
        return np.exp2(np.random.permutation(np.resize(levels, k // 32))).repeat(32)
    a = np.empty((k // 512, 16))
    for p in range(k // 512):
        a[p, :8] = np.random.permutation(np.resize(levels, 8))
        for g in range(8):
            far = levels[np.abs(levels - a[p, g]) >= 10]
            a[p, g + 8] = far[np.random.randint(len(far))]
    return np.exp2(a.ravel()).repeat(32)


def f64(x):
    return np.asarray(x).astype(np.float64)


def striped(idx):
    return np.tile(np.asarray(idx).reshape(-1, 16).T, (8, 1)).astype(np.uint16)


def unstriped(offs):
    return offs[:16].T.reshape(-1).astype(np.int64)


E2M1 = np.array([0.0, 0.5, 1.0, 1.5, 2.0, 3.0, 4.0, 6.0, -0.0, -0.5, -1.0, -1.5, -2.0, -3.0, -4.0, -6.0])


def pack_weight(w, fmt):
    k, n = w.shape
    w = f64(np.asarray(w, np.float32).astype(ml_dtypes.bfloat16)).reshape(k // 32, 32, n)
    amax = np.abs(w).max(1)
    if fmt == "e4m3":
        byte = np.frexp(amax)[1] - 1 + 127 - 7
    else:
        mant, ex = np.frexp(amax / 6.0)
        byte = np.where(mant > 0.5, ex, ex - 1) + 127
    byte = np.clip(np.where(amax > 0, byte, 1), 1, 254)
    scaled = (w * np.exp2(127.0 - byte)[:, None, :]).reshape(k, n).astype(np.float32)
    by_word = np.ascontiguousarray(scaled.reshape(k // 512, 128, 4, n).transpose(0, 1, 3, 2))
    if fmt == "e4m3":
        words = by_word.astype(ml_dtypes.float8_e4m3fn).view(np.uint8)
    else:
        c = by_word.astype(ml_dtypes.float4_e2m1fn).view(np.uint8) & 0xF
        words = (c[..., 0::2] | (c[..., 1::2] << 4)).reshape(k // 512, 128, 2 * n)
    return np.ascontiguousarray(words), np.ascontiguousarray(byte.astype(np.uint8).reshape(k // 512, 16, n))


def unpack_weight(words, scales, fmt):
    g, _, n = scales.shape
    words = np.ascontiguousarray(words).reshape(g, 128, n, -1)
    if fmt == "e4m3":
        vals = words.view(ml_dtypes.float8_e4m3fn).astype(np.float64)
    else:
        nib = np.empty((g, 128, n, 4), np.uint8)
        nib[..., 0::2] = words & 0xF
        nib[..., 1::2] = words >> 4
        vals = E2M1[nib]
    vals = vals * np.repeat(np.exp2(scales.astype(np.float64) - 127.0), 8, axis=1)[..., None]
    return vals.transpose(0, 1, 3, 2).reshape(g * 512, n)


D, E, T, I, Q, G = 512, 512, 2048, 512, 128, 64


def setup_inputs():
    n = np.random.standard_normal
    idx = np.random.permutation(T)[:I]
    fd = mx_kscale(D)
    fe = mx_kscale(E)
    keysp = pack_weight(n((D, T)) / fd[:, None], "e4m3")
    valsp = pack_weight(n((E, T)) / fe[:, None], "e4m3")
    return {
        "query": (n((D, Q)) * 0.7 / np.sqrt(D) * fd[:, None]).astype(np.float32),
        "keys_words": keysp[0],
        "keys_scales": keysp[1],
        "share": (np.random.uniform(0.2, 0.8, (Q, 1))).astype(np.float32),
        "gout": (n((E, Q)) * 1 / np.sqrt(E) * fe[:, None]).astype(np.float32),
        "vals_words": valsp[0],
        "vals_scales": valsp[1],
        "old": (0.5 * n((Q, T))).astype(np.float32),
        "offs": striped(idx),
    }


def reference(query, keys_words, keys_scales, share, gout, vals_words, vals_scales, old, offs):
    idx = unstriped(offs)
    keysu = unpack_weight(keys_words, keys_scales, "e4m3")
    valsu = unpack_weight(vals_words, vals_scales, "e4m3")
    queryq = mxq(f64(query), 0, "e4m3")
    keysidxg = keysu[:, idx]
    a = queryq.T @ keysidxg
    p = np.exp(a)
    z = np.sum(p, axis=1, keepdims=True)
    s = p.reshape(Q, G, I // G).sum(axis=2)
    v1 = 1.0 / (z * f64(share) + s * (1.0 - f64(share)) * 64.0)
    vr = np.repeat(v1, I // G, axis=1)
    goutq = mxq(f64(gout), 0, "e4m3")
    valsidxg = valsu[:, idx]
    c0 = goutq.T @ valsidxg
    dvr = c0 * p
    dv1 = dvr.reshape(Q, G, I // G).sum(axis=2)
    ds = dv1 * (-1.0) / np.square(z * f64(share) + s * (1.0 - f64(share)) * 64.0) * 64.0 * (1.0 - f64(share))
    r1 = np.repeat(ds, I // G, axis=1)
    dz = np.sum(dv1 * (-1.0) / np.square(z * f64(share) + s * (1.0 - f64(share)) * 64.0), axis=1, keepdims=True) * f64(share)
    dp = c0 * vr + r1 + dz
    da = dp * p
    gs = da * 512.0
    gf = np.zeros((Q, T))
    gf[:, idx] = gs
    y = f64(old) + gf
    return y

@@ -1,0 +1,182 @@
+from contextlib import ExitStack
+
+import concourse.mybir as mybir
+
+D, T, I, Q, G = 512, 2048, 512, 128, 64
+GROUP = I // G
+P = 128
+PACK = 4
+FLOPS = 2 * 2 * D * Q * I
+
+F32 = mybir.dt.float32
+BF16 = mybir.dt.bfloat16
+I32 = mybir.dt.int32
+U32 = mybir.dt.uint32
+U16 = mybir.dt.uint16
+U8 = mybir.dt.uint8
+FP8X4 = mybir.dt.float8_e4m3fn_x4
+ALU = mybir.AluOpType
+ACT = mybir.ActivationFunctionType
+AX = mybir.AxisListType
+
+KEY_ROW = 0
+VAL_ROW = 4
+OUT_CHUNKS = (256, 512, 512, 512, 256)
+
+
+def load_scale_rows(queue, window, scales, first_row):
+    for quad in range(4):
+        queue.dma_start(
+            out=window[32 * quad + first_row : 32 * quad + first_row + 4, :].bitcast(I32),
+            in_=scales[0, 4 * quad : 4 * quad + 4, :].bitcast(I32),
+        )
+
+
+def by_group(ap):
+    return ap.rearrange("p (g j) -> p g j", j=GROUP)
+
+
+def spread(ap):
+    return ap.unsqueeze(2).to_broadcast([P, G, GROUP])
+
+
+def tile_attend_bmixednorm_s_kernel(
+    tc, query, keys_words, keys_scales, share, gout, vals_words, vals_scales, old, offs, out
+):
+    nc = tc.nc
+    with ExitStack() as ctx:
+        sb = ctx.enter_context(tc.tile_pool(name="sb", bufs=1))
+        ps = ctx.enter_context(tc.psum_pool(name="ps", bufs=1))
+
+        offsets = sb.tile([P, I // 16], U16, name="offsets")
+        nc.sync.dma_start(offsets[:], offs)
+
+        ks_pool = sb.tile([P, T], U8, name="ks_pool", tag="chain", align_bytes=64)
+        vs_pool = sb.tile([P, T], U8, name="vs_pool", tag="vsp", align_bytes=64)
+        placed = sb.tile([P, T], F32, name="placed", align_bytes=64)
+        nc.vector.memset(ks_pool[:].bitcast(I32), 0)
+        nc.gpsimd.memset(vs_pool[:].bitcast(I32), 0)
+
+        load_scale_rows(nc.scalar, ks_pool, keys_scales, KEY_ROW)
+        kw_pool = sb.tile([P, T], U32, name="kw_pool", tag="big", align_bytes=64)
+        nc.sync.dma_start(
+            out=kw_pool[:].bitcast(I32), in_=keys_words[0].rearrange("p n t -> p (n t)").bitcast(I32)
+        )
+        q_raw = sb.tile([P, PACK, Q], F32, name="q_raw", tag="raw")
+        nc.sync.dma_start(out=q_raw[:], in_=query.rearrange("(p j) w -> p j w", j=PACK))
+        vw_pool = sb.tile([P, T], U32, name="vw_pool", tag="big2", align_bytes=64)
+        nc.sync.dma_start(
+            out=vw_pool[:].bitcast(I32), in_=vals_words[0].rearrange("p n t -> p (n t)").bitcast(I32)
+        )
+        load_scale_rows(nc.gpsimd, vs_pool, vals_scales, VAL_ROW)
+        sh = sb.tile([P, 1], F32, name="sh")
+        nc.gpsimd.dma_start(out=sh[:], in_=share)
+        nc.vector.memset(placed[:, : T // 2 - 1], 0.0)
+        nc.vector.memset(placed[:, T // 2 - 1 :], 0.0)
+
+        ks = sb.tile([P, I], U8, name="ks", align_bytes=64)
+        nc.vector.tensor_copy(ks[:], ks_pool[:].indirect(offsets[:]))
+        kw = sb.tile([P, I], U32, name="kw", tag="chain", align_bytes=64)
+        nc.vector.tensor_copy(kw[:], kw_pool[:].indirect(offsets[:]))
+        q_bf = sb.tile([P, Q, PACK], BF16, name="q_bf", align_bytes=64)
+        nc.scalar.copy(out=q_bf[:], in_=q_raw[:].rearrange("p j w -> p w j"))
+        q_codes = sb.tile([P, Q], U32, name="q_codes", align_bytes=64)
+        q_scales = sb.tile([P, Q], U8, name="q_scales", align_bytes=64)
+        nc.vector.quantize_mx(
+            out=q_codes[:].bitcast(FP8X4), scales=q_scales[:], in_=q_bf[:].rearrange("p w j -> p (w j)")
+        )
+        g_raw = sb.tile([P, PACK, Q], F32, name="g_raw", tag="raw")
+        nc.sync.dma_start(out=g_raw[:], in_=gout.rearrange("(p j) w -> p j w", j=PACK))
+
+
+        a = ps.tile([P, I], F32, name="a")
+        nc.tensor.matmul_mx(
+            out=a[:],
+            lhsT=q_codes[:].bitcast(FP8X4),
+            lhsT_scale=q_scales[:],
+            rhs=kw[:].bitcast(FP8X4),
+            rhs_scale=ks[KEY_ROW:P, :],
+            start=True,
+            stop=True,
+        )
+        vs = sb.tile([P, I], U8, name="vs", tag="big", align_bytes=64)
+        nc.vector.tensor_copy(vs[:], vs_pool[:].indirect(offsets[:]))
+
+        neg_max = sb.tile([P, 1], F32, name="neg_max", tag="vsp", align_bytes=64)
+        nc.vector.tensor_reduce(out=neg_max[:], in_=a[:], axis=AX.X, op=ALU.max, negate=True)
+        p = sb.tile([P, I], F32, name="p")
+        z = sb.tile([P, 1], F32, name="z")
+        nc.scalar.activation(out=p[:], in_=a[:], func=ACT.Exp, bias=neg_max[:], scale=1.0, accum_out=z[:])
+        z_share = sb.tile([P, 1], F32, name="z_share")
+        nc.scalar.activation(out=z_share[:], in_=z[:], func=ACT.Copy, scale=sh[:])
+        rest = sb.tile([P, 1], F32, name="rest")
+        nc.gpsimd.tensor_scalar(
+            out=rest[:], in0=sh[:], scalar1=-64.0, scalar2=64.0, op0=ALU.mult, op1=ALU.add
+        )
+
+        vw = sb.tile([P, I], U32, name="vw", tag="chain", align_bytes=64)
+        nc.vector.tensor_copy(vw[:], vw_pool[:].indirect(offsets[:]))
+        prior = sb.tile([P, T], F32, name="prior", tag="big2", align_bytes=64)
+        nc.sync.dma_start(out=prior[:], in_=old)
+        g_bf = sb.tile([P, Q, PACK], BF16, name="g_bf", align_bytes=64)
+        nc.scalar.copy(out=g_bf[:], in_=g_raw[:].rearrange("p j w -> p w j"))
+        g_codes = sb.tile([P, Q], U32, name="g_codes", align_bytes=64)
+        g_scales = sb.tile([P, Q], U8, name="g_scales", align_bytes=64)
+        nc.vector.quantize_mx(
+            out=g_codes[:].bitcast(FP8X4), scales=g_scales[:], in_=g_bf[:].rearrange("p w j -> p (w j)")
+        )
+        c0 = ps.tile([P, I], F32, name="c0")
+        nc.tensor.matmul_mx(
+            out=c0[:],
+            lhsT=g_codes[:].bitcast(FP8X4),
+            lhsT_scale=g_scales[:],
+            rhs=vw[:].bitcast(FP8X4),
+            rhs_scale=vs[VAL_ROW:P, :],
+            start=True,
+            stop=True,
+        )
+
+        s = sb.tile([P, G], F32, name="s")
+        nc.vector.tensor_reduce(out=s[:], in_=by_group(p[:]), axis=AX.X, op=ALU.add)
+        den = sb.tile([P, G], F32, name="den")
+        nc.vector.tensor_scalar(
+            out=den[:], in0=s[:], scalar1=rest[:], scalar2=z_share[:], op0=ALU.mult, op1=ALU.add
+        )
+        dvr = sb.tile([P, I], F32, name="dvr")
+        nc.vector.tensor_tensor(out=dvr[:], in0=c0[:], in1=p[:], op=ALU.mult)
+        v1 = sb.tile([P, G], F32, name="v1")
+        nc.vector.reciprocal(out=v1[:], in_=den[:])
+        dv1 = sb.tile([P, G], F32, name="dv1")
+        nc.vector.tensor_reduce(out=dv1[:], in_=by_group(dvr[:]), axis=AX.X, op=ALU.add)
+        v1_sq = sb.tile([P, G], F32, name="v1_sq")
+        nc.scalar.activation(out=v1_sq[:], in_=v1[:], func=ACT.Square)
+        weight = sb.tile([P, I], F32, name="weight")
+        nc.vector.scalar_tensor_tensor(
+            out=by_group(weight[:]), in0=by_group(p[:]), scalar=512.0, in1=spread(v1[:]), op0=ALU.mult, op1=ALU.mult
+        )
+        row_terms = sb.tile([P, G], F32, name="row_terms")
+        neg_dz = sb.tile([P, 1], F32, name="neg_dz")
+        nc.vector.scalar_tensor_tensor(
+            out=row_terms[:], in0=dv1[:], scalar=sh[:], in1=v1_sq[:], op0=ALU.mult, op1=ALU.mult, accum_out=neg_dz[:]
+        )
+        group_term = sb.tile([P, G], F32, name="group_term")
+        nc.vector.scalar_tensor_tensor(
+            out=group_term[:], in0=dv1[:], scalar=rest[:], in1=v1[:], op0=ALU.mult, op1=ALU.mult
+        )
+        shift = sb.tile([P, G], F32, name="shift")
+        nc.vector.scalar_tensor_tensor(
+            out=shift[:], in0=den[:], scalar=neg_dz[:], in1=group_term[:], op0=ALU.mult, op1=ALU.add
+        )
+        centred = sb.tile([P, I], F32, name="centred")
+        nc.vector.tensor_tensor(
+            out=by_group(centred[:]), in0=by_group(c0[:]), in1=spread(shift[:]), op=ALU.subtract
+        )
+        nc.vector.tensor_tensor(placed[:].indirect(offsets[:]), centred[:], weight[:], ALU.mult)
+
+        col = 0
+        for n, width in enumerate(OUT_CHUNKS):
+            cols = slice(col, col + width)
+            total = sb.tile([P, width], F32, name="total%d" % n)
+            nc.vector.tensor_tensor(out=total[:], in0=prior[:, cols], in1=placed[:, cols], op=ALU.add)
+            nc.sync.dma_start(out=out[:, cols], in_=total[:])
+            col += width

@@ -21,7 +21,8 @@ AX = mybir.AxisListType
 
 KEY_ROW = 0
 VAL_ROW = 4
-OUT_CHUNKS = (256, 512, 512, 512, 256)
+HALF = I // 2
+OUT_CHUNKS = (320, 448, 448, 384, 320, 128)
 
 
 def load_scale_rows(queue, window, scales, first_row):
@@ -32,12 +33,18 @@ def load_scale_rows(queue, window, scales, first_row):
         )
 
 
+def zero_in_odd_runs(nc, ap, zero):
+    cut = ap.shape[1] // 2 - 1
+    nc.vector.memset(ap[:, :cut], zero)
+    nc.vector.memset(ap[:, cut:], zero)
+
+
 def by_group(ap):
     return ap.rearrange("p (g j) -> p g j", j=GROUP)
 
 
 def spread(ap):
-    return ap.unsqueeze(2).to_broadcast([P, G, GROUP])
+    return ap.unsqueeze(2).to_broadcast([P, ap.shape[1], GROUP])
 
 
 def tile_attend_bmixednorm_s_kernel(
@@ -51,43 +58,56 @@ def tile_attend_bmixednorm_s_kernel(
         offsets = sb.tile([P, I // 16], U16, name="offsets")
         nc.sync.dma_start(offsets[:], offs)
 
-        ks_pool = sb.tile([P, T], U8, name="ks_pool", tag="chain", align_bytes=64)
-        vs_pool = sb.tile([P, T], U8, name="vs_pool", tag="vsp", align_bytes=64)
+        ks_pool = sb.tile([P, T], U8, name="ks_pool", tag="keys_chain", align_bytes=64)
+        vs_pool = sb.tile([P, T], U8, name="vs_pool", align_bytes=64)
         placed = sb.tile([P, T], F32, name="placed", align_bytes=64)
-        nc.vector.memset(ks_pool[:].bitcast(I32), 0)
-        nc.gpsimd.memset(vs_pool[:].bitcast(I32), 0)
+        nc.gpsimd.memset(ks_pool[:].bitcast(I32), 0)
+        zero_in_odd_runs(nc, vs_pool[:].bitcast(I32), 0)
+        sh = sb.tile([P, 1], F32, name="sh")
+        nc.sync.dma_start(out=sh[:], in_=share)
 
-        load_scale_rows(nc.scalar, ks_pool, keys_scales, KEY_ROW)
-        kw_pool = sb.tile([P, T], U32, name="kw_pool", tag="big", align_bytes=64)
+        load_scale_rows(nc.sync, ks_pool, keys_scales, KEY_ROW)
+        kw_pool = sb.tile([P, T], U32, name="kw_pool", tag="kw_vs_v1", align_bytes=64)
         nc.sync.dma_start(
             out=kw_pool[:].bitcast(I32), in_=keys_words[0].rearrange("p n t -> p (n t)").bitcast(I32)
         )
-        q_raw = sb.tile([P, PACK, Q], F32, name="q_raw", tag="raw")
+        q_raw = sb.tile([P, PACK, Q], F32, name="q_raw")
         nc.sync.dma_start(out=q_raw[:], in_=query.rearrange("(p j) w -> p j w", j=PACK))
-        vw_pool = sb.tile([P, T], U32, name="vw_pool", tag="big2", align_bytes=64)
+        load_scale_rows(nc.sync, vs_pool, vals_scales, VAL_ROW)
+        g_raw = sb.tile([P, PACK, Q], F32, name="g_raw")
+        nc.sync.dma_start(out=g_raw[:], in_=gout.rearrange("(p j) w -> p j w", j=PACK))
+        vw_pool = sb.tile([P, T], U32, name="vw_pool", align_bytes=64)
         nc.sync.dma_start(
             out=vw_pool[:].bitcast(I32), in_=vals_words[0].rearrange("p n t -> p (n t)").bitcast(I32)
         )
-        load_scale_rows(nc.gpsimd, vs_pool, vals_scales, VAL_ROW)
-        sh = sb.tile([P, 1], F32, name="sh")
-        nc.gpsimd.dma_start(out=sh[:], in_=share)
-        nc.vector.memset(placed[:, : T // 2 - 1], 0.0)
-        nc.vector.memset(placed[:, T // 2 - 1 :], 0.0)
+        prior = sb.tile([P, T], F32, name="prior", align_bytes=64)
+        nc.sync.dma_start(out=prior[:], in_=old)
+        zero_in_odd_runs(nc, placed[:], 0.0)
 
-        ks = sb.tile([P, I], U8, name="ks", align_bytes=64)
+        halves = [slice(h * HALF, (h + 1) * HALF) for h in range(2)]
+        group_halves = [slice(h * G // 2, (h + 1) * G // 2) for h in range(2)]
+        list_halves = [offsets[:, h * HALF // 16 : (h + 1) * HALF // 16] for h in range(2)]
+
+        ks = sb.tile([P, I], U8, name="ks", tag="ks_then_vs", align_bytes=64)
         nc.vector.tensor_copy(ks[:], ks_pool[:].indirect(offsets[:]))
-        kw = sb.tile([P, I], U32, name="kw", tag="chain", align_bytes=64)
+        kw = sb.tile([P, I], U32, name="kw", tag="keys_chain", align_bytes=64)
         nc.vector.tensor_copy(kw[:], kw_pool[:].indirect(offsets[:]))
         q_bf = sb.tile([P, Q, PACK], BF16, name="q_bf", align_bytes=64)
         nc.scalar.copy(out=q_bf[:], in_=q_raw[:].rearrange("p j w -> p w j"))
+        g_bf = sb.tile([P, Q, PACK], BF16, name="g_bf", align_bytes=64)
+        nc.scalar.copy(out=g_bf[:], in_=g_raw[:].rearrange("p j w -> p w j"))
         q_codes = sb.tile([P, Q], U32, name="q_codes", align_bytes=64)
         q_scales = sb.tile([P, Q], U8, name="q_scales", align_bytes=64)
         nc.vector.quantize_mx(
             out=q_codes[:].bitcast(FP8X4), scales=q_scales[:], in_=q_bf[:].rearrange("p w j -> p (w j)")
         )
-        g_raw = sb.tile([P, PACK, Q], F32, name="g_raw", tag="raw")
-        nc.sync.dma_start(out=g_raw[:], in_=gout.rearrange("(p j) w -> p j w", j=PACK))
-
+        vs_lo = sb.tile([P, HALF], U8, name="vs_lo", tag="kw_vs_v1", align_bytes=64)
+        nc.vector.tensor_copy(vs_lo[:], vs_pool[:].indirect(list_halves[0]))
+        g_codes = sb.tile([P, Q], U32, name="g_codes", align_bytes=64)
+        g_scales = sb.tile([P, Q], U8, name="g_scales", align_bytes=64)
+        nc.vector.quantize_mx(
+            out=g_codes[:].bitcast(FP8X4), scales=g_scales[:], in_=g_bf[:].rearrange("p w j -> p (w j)")
+        )
 
         a = ps.tile([P, I], F32, name="a")
         nc.tensor.matmul_mx(
@@ -99,79 +119,85 @@ def tile_attend_bmixednorm_s_kernel(
             start=True,
             stop=True,
         )
-        vs = sb.tile([P, I], U8, name="vs", tag="big", align_bytes=64)
-        nc.vector.tensor_copy(vs[:], vs_pool[:].indirect(offsets[:]))
 
-        neg_max = sb.tile([P, 1], F32, name="neg_max", tag="vsp", align_bytes=64)
+        neg_max = sb.tile([P, 1], F32, name="neg_max", tag="keys_chain", align_bytes=64)
         nc.vector.tensor_reduce(out=neg_max[:], in_=a[:], axis=AX.X, op=ALU.max, negate=True)
+        vs_hi = sb.tile([P, HALF], U8, name="vs_hi", tag="ks_then_vs", align_bytes=64)
+        nc.vector.tensor_copy(vs_hi[:], vs_pool[:].indirect(list_halves[1]))
         p = sb.tile([P, I], F32, name="p")
-        z = sb.tile([P, 1], F32, name="z")
-        nc.scalar.activation(out=p[:], in_=a[:], func=ACT.Exp, bias=neg_max[:], scale=1.0, accum_out=z[:])
+        s = sb.tile([P, G], F32, name="s")
+        z_halves = sb.tile([P, 2], F32, name="z_halves")
+        for h, (cols, groups) in enumerate(zip(halves, group_halves)):
+            nc.scalar.activation(
+                out=p[:, cols], in_=a[:, cols], func=ACT.Exp, bias=neg_max[:], scale=1.0, accum_out=z_halves[:, h : h + 1]
+            )
+            nc.vector.tensor_reduce(out=s[:, groups], in_=by_group(p[:, cols]), axis=AX.X, op=ALU.add)
+        z_halves_share = sb.tile([P, 2], F32, name="z_halves_share")
         z_share = sb.tile([P, 1], F32, name="z_share")
-        nc.scalar.activation(out=z_share[:], in_=z[:], func=ACT.Copy, scale=sh[:])
+        nc.scalar.activation(out=z_halves_share[:], in_=z_halves[:], func=ACT.Copy, scale=sh[:], accum_out=z_share[:])
         rest = sb.tile([P, 1], F32, name="rest")
         nc.gpsimd.tensor_scalar(
             out=rest[:], in0=sh[:], scalar1=-64.0, scalar2=64.0, op0=ALU.mult, op1=ALU.add
         )
-
-        vw = sb.tile([P, I], U32, name="vw", tag="chain", align_bytes=64)
-        nc.vector.tensor_copy(vw[:], vw_pool[:].indirect(offsets[:]))
-        prior = sb.tile([P, T], F32, name="prior", tag="big2", align_bytes=64)
-        nc.sync.dma_start(out=prior[:], in_=old)
-        g_bf = sb.tile([P, Q, PACK], BF16, name="g_bf", align_bytes=64)
-        nc.scalar.copy(out=g_bf[:], in_=g_raw[:].rearrange("p j w -> p w j"))
-        g_codes = sb.tile([P, Q], U32, name="g_codes", align_bytes=64)
-        g_scales = sb.tile([P, Q], U8, name="g_scales", align_bytes=64)
-        nc.vector.quantize_mx(
-            out=g_codes[:].bitcast(FP8X4), scales=g_scales[:], in_=g_bf[:].rearrange("p w j -> p (w j)")
+        group_factor = sb.tile([P, 1], F32, name="group_factor")
+        nc.gpsimd.tensor_scalar(
+            out=group_factor[:], in0=sh[:], scalar1=32768.0, scalar2=-32768.0, op0=ALU.mult, op1=ALU.add
         )
-        c0 = ps.tile([P, I], F32, name="c0")
-        nc.tensor.matmul_mx(
-            out=c0[:],
-            lhsT=g_codes[:].bitcast(FP8X4),
-            lhsT_scale=g_scales[:],
-            rhs=vw[:].bitcast(FP8X4),
-            rhs_scale=vs[VAL_ROW:P, :],
-            start=True,
-            stop=True,
+        row_factor = sb.tile([P, 1], F32, name="row_factor")
+        nc.gpsimd.tensor_scalar(
+            out=row_factor[:], in0=sh[:], scalar1=-512.0, scalar2=0.0, op0=ALU.mult, op1=ALU.add
         )
-
-        s = sb.tile([P, G], F32, name="s")
-        nc.vector.tensor_reduce(out=s[:], in_=by_group(p[:]), axis=AX.X, op=ALU.add)
         den = sb.tile([P, G], F32, name="den")
-        nc.vector.tensor_scalar(
-            out=den[:], in0=s[:], scalar1=rest[:], scalar2=z_share[:], op0=ALU.mult, op1=ALU.add
-        )
-        dvr = sb.tile([P, I], F32, name="dvr")
-        nc.vector.tensor_tensor(out=dvr[:], in0=c0[:], in1=p[:], op=ALU.mult)
+        nc.scalar.activation(out=den[:], in_=s[:], func=ACT.Identity, scale=rest[:], bias=z_share[:])
+
+        vw = sb.tile([P, I], U32, name="vw", tag="keys_chain", align_bytes=64)
+        c0 = [ps.tile([P, HALF], F32, name="c0_%d" % h) for h in range(2)]
+        for cols, entries, vs, bank in zip(halves, list_halves, (vs_lo, vs_hi), c0):
+            nc.vector.tensor_copy(vw[:, cols], vw_pool[:].indirect(entries))
+            nc.tensor.matmul_mx(
+                out=bank[:],
+                lhsT=g_codes[:].bitcast(FP8X4),
+                lhsT_scale=g_scales[:],
+                rhs=vw[:, cols].bitcast(FP8X4),
+                rhs_scale=vs[VAL_ROW:P, :],
+                start=True,
+                stop=True,
+            )
+
         v1 = sb.tile([P, G], F32, name="v1")
         nc.vector.reciprocal(out=v1[:], in_=den[:])
-        dv1 = sb.tile([P, G], F32, name="dv1")
-        nc.vector.tensor_reduce(out=dv1[:], in_=by_group(dvr[:]), axis=AX.X, op=ALU.add)
         v1_sq = sb.tile([P, G], F32, name="v1_sq")
         nc.scalar.activation(out=v1_sq[:], in_=v1[:], func=ACT.Square)
-        weight = sb.tile([P, I], F32, name="weight")
-        nc.vector.scalar_tensor_tensor(
-            out=by_group(weight[:]), in0=by_group(p[:]), scalar=512.0, in1=spread(v1[:]), op0=ALU.mult, op1=ALU.mult
-        )
+        dvr = sb.tile([P, I], F32, name="dvr")
+        dv1 = sb.tile([P, G], F32, name="dv1")
+        for cols, bank in zip(halves, c0):
+            nc.vector.tensor_tensor(out=dvr[:, cols], in0=bank[:], in1=p[:, cols], op=ALU.mult)
+        for cols, groups in zip(halves, group_halves):
+            nc.vector.tensor_reduce(out=dv1[:, groups], in_=by_group(dvr[:, cols]), axis=AX.X, op=ALU.add)
         row_terms = sb.tile([P, G], F32, name="row_terms")
-        neg_dz = sb.tile([P, 1], F32, name="neg_dz")
+        dz = sb.tile([P, 1], F32, name="dz")
         nc.vector.scalar_tensor_tensor(
-            out=row_terms[:], in0=dv1[:], scalar=sh[:], in1=v1_sq[:], op0=ALU.mult, op1=ALU.mult, accum_out=neg_dz[:]
+            out=row_terms[:], in0=dv1[:], scalar=row_factor[:], in1=v1_sq[:], op0=ALU.mult, op1=ALU.mult, accum_out=dz[:]
         )
-        group_term = sb.tile([P, G], F32, name="group_term")
+        ds = sb.tile([P, G], F32, name="ds")
         nc.vector.scalar_tensor_tensor(
-            out=group_term[:], in0=dv1[:], scalar=rest[:], in1=v1[:], op0=ALU.mult, op1=ALU.mult
+            out=ds[:], in0=dv1[:], scalar=group_factor[:], in1=v1_sq[:], op0=ALU.mult, op1=ALU.mult
         )
-        shift = sb.tile([P, G], F32, name="shift")
+        through_sums = sb.tile([P, I], F32, name="through_sums")
         nc.vector.scalar_tensor_tensor(
-            out=shift[:], in0=den[:], scalar=neg_dz[:], in1=group_term[:], op0=ALU.mult, op1=ALU.add
+            out=by_group(through_sums[:]), in0=spread(ds[:]), scalar=dz[:], in1=by_group(p[:]), op0=ALU.add, op1=ALU.mult
         )
-        centred = sb.tile([P, I], F32, name="centred")
-        nc.vector.tensor_tensor(
-            out=by_group(centred[:]), in0=by_group(c0[:]), in1=spread(shift[:]), op=ALU.subtract
-        )
-        nc.vector.tensor_tensor(placed[:].indirect(offsets[:]), centred[:], weight[:], ALU.mult)
+        direct = sb.tile([P, I], F32, name="direct")
+        for cols, groups in zip(halves, group_halves):
+            nc.vector.scalar_tensor_tensor(
+                out=by_group(direct[:, cols]),
+                in0=by_group(dvr[:, cols]),
+                scalar=512.0,
+                in1=spread(v1[:, groups]),
+                op0=ALU.mult,
+                op1=ALU.mult,
+            )
+        nc.vector.tensor_tensor(placed[:].indirect(offsets[:]), direct[:], through_sums[:], ALU.add)
 
         col = 0
         for n, width in enumerate(OUT_CHUNKS):

@@ -26,17 +26,11 @@ OUT_CHUNKS = (320, 448, 448, 384, 320, 128)
 
 
 def load_scale_rows(queue, window, scales, first_row):
-    for quad in range(4):
+    for quad in (0, 2, 1, 3):
         queue.dma_start(
             out=window[32 * quad + first_row : 32 * quad + first_row + 4, :].bitcast(I32),
             in_=scales[0, 4 * quad : 4 * quad + 4, :].bitcast(I32),
         )
-
-
-def zero_in_odd_runs(nc, ap, zero):
-    cut = ap.shape[1] // 2 - 1
-    nc.vector.memset(ap[:, :cut], zero)
-    nc.vector.memset(ap[:, cut:], zero)
 
 
 def by_group(ap):
@@ -62,19 +56,19 @@ def tile_attend_bmixednorm_s_kernel(
         vs_pool = sb.tile([P, T], U8, name="vs_pool", align_bytes=64)
         placed = sb.tile([P, T], F32, name="placed", align_bytes=64)
         nc.gpsimd.memset(ks_pool[:].bitcast(I32), 0)
-        zero_in_odd_runs(nc, vs_pool[:].bitcast(I32), 0)
+        nc.vector.memset(vs_pool[:].bitcast(I32), 0)
         sh = sb.tile([P, 1], F32, name="sh")
-        nc.sync.dma_start(out=sh[:], in_=share)
+        nc.gpsimd.dma_start(out=sh[:], in_=share)
+        q_raw = sb.tile([P, PACK, Q], F32, name="q_raw")
+        nc.sync.dma_start(out=q_raw[:], in_=query.rearrange("(p j) w -> p j w", j=PACK))
 
         load_scale_rows(nc.sync, ks_pool, keys_scales, KEY_ROW)
-        kw_pool = sb.tile([P, T], U32, name="kw_pool", tag="kw_vs_v1", align_bytes=64)
+        kw_pool = sb.tile([P, T], U32, name="kw_pool", align_bytes=64)
         nc.sync.dma_start(
             out=kw_pool[:].bitcast(I32), in_=keys_words[0].rearrange("p n t -> p (n t)").bitcast(I32)
         )
-        q_raw = sb.tile([P, PACK, Q], F32, name="q_raw")
-        nc.sync.dma_start(out=q_raw[:], in_=query.rearrange("(p j) w -> p j w", j=PACK))
         load_scale_rows(nc.sync, vs_pool, vals_scales, VAL_ROW)
-        g_raw = sb.tile([P, PACK, Q], F32, name="g_raw")
+        g_raw = sb.tile([P, PACK, Q], F32, name="g_raw", tag="g_then_p")
         nc.sync.dma_start(out=g_raw[:], in_=gout.rearrange("(p j) w -> p j w", j=PACK))
         vw_pool = sb.tile([P, T], U32, name="vw_pool", align_bytes=64)
         nc.sync.dma_start(
@@ -82,7 +76,7 @@ def tile_attend_bmixednorm_s_kernel(
         )
         prior = sb.tile([P, T], F32, name="prior", align_bytes=64)
         nc.sync.dma_start(out=prior[:], in_=old)
-        zero_in_odd_runs(nc, placed[:], 0.0)
+        nc.vector.memset(placed[:], 0.0)
 
         halves = [slice(h * HALF, (h + 1) * HALF) for h in range(2)]
         group_halves = [slice(h * G // 2, (h + 1) * G // 2) for h in range(2)]
@@ -91,40 +85,40 @@ def tile_attend_bmixednorm_s_kernel(
         ks = sb.tile([P, I], U8, name="ks", tag="ks_then_vs", align_bytes=64)
         nc.vector.tensor_copy(ks[:], ks_pool[:].indirect(offsets[:]))
         kw = sb.tile([P, I], U32, name="kw", tag="keys_chain", align_bytes=64)
-        nc.vector.tensor_copy(kw[:], kw_pool[:].indirect(offsets[:]))
         q_bf = sb.tile([P, Q, PACK], BF16, name="q_bf", align_bytes=64)
         nc.scalar.copy(out=q_bf[:], in_=q_raw[:].rearrange("p j w -> p w j"))
         g_bf = sb.tile([P, Q, PACK], BF16, name="g_bf", align_bytes=64)
         nc.scalar.copy(out=g_bf[:], in_=g_raw[:].rearrange("p j w -> p w j"))
-        q_codes = sb.tile([P, Q], U32, name="q_codes", align_bytes=64)
+        q_codes = sb.tile([P, Q], U32, name="q_codes", tag="row_codes", align_bytes=64)
         q_scales = sb.tile([P, Q], U8, name="q_scales", align_bytes=64)
         nc.vector.quantize_mx(
             out=q_codes[:].bitcast(FP8X4), scales=q_scales[:], in_=q_bf[:].rearrange("p w j -> p (w j)")
         )
-        vs_lo = sb.tile([P, HALF], U8, name="vs_lo", tag="kw_vs_v1", align_bytes=64)
-        nc.vector.tensor_copy(vs_lo[:], vs_pool[:].indirect(list_halves[0]))
-        g_codes = sb.tile([P, Q], U32, name="g_codes", align_bytes=64)
-        g_scales = sb.tile([P, Q], U8, name="g_scales", align_bytes=64)
-        nc.vector.quantize_mx(
-            out=g_codes[:].bitcast(FP8X4), scales=g_scales[:], in_=g_bf[:].rearrange("p w j -> p (w j)")
-        )
-
         a = ps.tile([P, I], F32, name="a")
-        nc.tensor.matmul_mx(
-            out=a[:],
-            lhsT=q_codes[:].bitcast(FP8X4),
-            lhsT_scale=q_scales[:],
-            rhs=kw[:].bitcast(FP8X4),
-            rhs_scale=ks[KEY_ROW:P, :],
-            start=True,
-            stop=True,
-        )
+        for cols, entries in zip(halves, list_halves):
+            nc.vector.tensor_copy(kw[:, cols], kw_pool[:].indirect(entries))
+            nc.tensor.matmul_mx(
+                out=a[:, cols],
+                lhsT=q_codes[:].bitcast(FP8X4),
+                lhsT_scale=q_scales[:],
+                rhs=kw[:, cols].bitcast(FP8X4),
+                rhs_scale=ks[KEY_ROW:P, cols],
+                start=True,
+                stop=True,
+            )
+        vs_lo = sb.tile([P, HALF], U8, name="vs_lo", align_bytes=64)
+        nc.vector.tensor_copy(vs_lo[:], vs_pool[:].indirect(list_halves[0]))
 
         neg_max = sb.tile([P, 1], F32, name="neg_max", tag="keys_chain", align_bytes=64)
         nc.vector.tensor_reduce(out=neg_max[:], in_=a[:], axis=AX.X, op=ALU.max, negate=True)
         vs_hi = sb.tile([P, HALF], U8, name="vs_hi", tag="ks_then_vs", align_bytes=64)
         nc.vector.tensor_copy(vs_hi[:], vs_pool[:].indirect(list_halves[1]))
-        p = sb.tile([P, I], F32, name="p")
+        g_codes = sb.tile([P, Q], U32, name="g_codes", tag="row_codes", align_bytes=64)
+        g_scales = sb.tile([P, Q], U8, name="g_scales", align_bytes=64)
+        nc.vector.quantize_mx(
+            out=g_codes[:].bitcast(FP8X4), scales=g_scales[:], in_=g_bf[:].rearrange("p w j -> p (w j)")
+        )
+        p = sb.tile([P, I], F32, name="p", tag="g_then_p")
         s = sb.tile([P, G], F32, name="s")
         z_halves = sb.tile([P, 2], F32, name="z_halves")
         for h, (cols, groups) in enumerate(zip(halves, group_halves)):

from contextlib import ExitStack

import concourse.mybir as mybir

D, T, I, Q, G = 512, 2048, 512, 128, 64
GROUP = I // G
P = 128
PACK = 4
FLOPS = 2 * 2 * D * Q * I

F32 = mybir.dt.float32
BF16 = mybir.dt.bfloat16
I32 = mybir.dt.int32
U32 = mybir.dt.uint32
U16 = mybir.dt.uint16
U8 = mybir.dt.uint8
FP8X4 = mybir.dt.float8_e4m3fn_x4
ALU = mybir.AluOpType
ACT = mybir.ActivationFunctionType
AX = mybir.AxisListType

KEY_ROW = 0
VAL_ROW = 4
HALF = I // 2
OUT_CHUNKS = (320, 448, 448, 384, 320, 128)


def load_scale_rows(queue, window, scales, first_row):
    for quad in (0, 2, 1, 3):
        queue.dma_start(
            out=window[32 * quad + first_row : 32 * quad + first_row + 4, :].bitcast(I32),
            in_=scales[0, 4 * quad : 4 * quad + 4, :].bitcast(I32),
        )


def by_group(ap):
    return ap.rearrange("p (g j) -> p g j", j=GROUP)


def spread(ap):
    return ap.unsqueeze(2).to_broadcast([P, ap.shape[1], GROUP])


def tile_attend_bmixednorm_s_kernel(
    tc, query, keys_words, keys_scales, share, gout, vals_words, vals_scales, old, offs, out
):
    nc = tc.nc
    with ExitStack() as ctx:
        sb = ctx.enter_context(tc.tile_pool(name="sb", bufs=1))
        ps = ctx.enter_context(tc.psum_pool(name="ps", bufs=1))

        offsets = sb.tile([P, I // 16], U16, name="offsets")
        nc.sync.dma_start(offsets[:], offs)

        ks_pool = sb.tile([P, T], U8, name="ks_pool", tag="keys_chain", align_bytes=64)
        vs_pool = sb.tile([P, T], U8, name="vs_pool", align_bytes=64)
        placed = sb.tile([P, T], F32, name="placed", align_bytes=64)
        nc.gpsimd.memset(ks_pool[:].bitcast(I32), 0)
        nc.vector.memset(vs_pool[:].bitcast(I32), 0)
        sh = sb.tile([P, 1], F32, name="sh")
        nc.gpsimd.dma_start(out=sh[:], in_=share)
        q_raw = sb.tile([P, PACK, Q], F32, name="q_raw")
        nc.sync.dma_start(out=q_raw[:], in_=query.rearrange("(p j) w -> p j w", j=PACK))

        load_scale_rows(nc.sync, ks_pool, keys_scales, KEY_ROW)
        kw_pool = sb.tile([P, T], U32, name="kw_pool", align_bytes=64)
        nc.sync.dma_start(
            out=kw_pool[:].bitcast(I32), in_=keys_words[0].rearrange("p n t -> p (n t)").bitcast(I32)
        )
        load_scale_rows(nc.sync, vs_pool, vals_scales, VAL_ROW)
        g_raw = sb.tile([P, PACK, Q], F32, name="g_raw", tag="g_then_p")
        nc.sync.dma_start(out=g_raw[:], in_=gout.rearrange("(p j) w -> p j w", j=PACK))
        vw_pool = sb.tile([P, T], U32, name="vw_pool", align_bytes=64)
        nc.sync.dma_start(
            out=vw_pool[:].bitcast(I32), in_=vals_words[0].rearrange("p n t -> p (n t)").bitcast(I32)
        )
        prior = sb.tile([P, T], F32, name="prior", align_bytes=64)
        nc.sync.dma_start(out=prior[:], in_=old)
        nc.vector.memset(placed[:], 0.0)

        halves = [slice(h * HALF, (h + 1) * HALF) for h in range(2)]
        group_halves = [slice(h * G // 2, (h + 1) * G // 2) for h in range(2)]
        list_halves = [offsets[:, h * HALF // 16 : (h + 1) * HALF // 16] for h in range(2)]

        ks = sb.tile([P, I], U8, name="ks", tag="ks_then_vs", align_bytes=64)
        nc.vector.tensor_copy(ks[:], ks_pool[:].indirect(offsets[:]))
        kw = sb.tile([P, I], U32, name="kw", tag="keys_chain", align_bytes=64)
        q_bf = sb.tile([P, Q, PACK], BF16, name="q_bf", align_bytes=64)
        nc.scalar.copy(out=q_bf[:], in_=q_raw[:].rearrange("p j w -> p w j"))
        g_bf = sb.tile([P, Q, PACK], BF16, name="g_bf", align_bytes=64)
        nc.scalar.copy(out=g_bf[:], in_=g_raw[:].rearrange("p j w -> p w j"))
        q_codes = sb.tile([P, Q], U32, name="q_codes", tag="row_codes", align_bytes=64)
        q_scales = sb.tile([P, Q], U8, name="q_scales", align_bytes=64)
        nc.vector.quantize_mx(
            out=q_codes[:].bitcast(FP8X4), scales=q_scales[:], in_=q_bf[:].rearrange("p w j -> p (w j)")
        )
        a = ps.tile([P, I], F32, name="a")
        for cols, entries in zip(halves, list_halves):
            nc.vector.tensor_copy(kw[:, cols], kw_pool[:].indirect(entries))
            nc.tensor.matmul_mx(
                out=a[:, cols],
                lhsT=q_codes[:].bitcast(FP8X4),
                lhsT_scale=q_scales[:],
                rhs=kw[:, cols].bitcast(FP8X4),
                rhs_scale=ks[KEY_ROW:P, cols],
                start=True,
                stop=True,
            )
        vs_lo = sb.tile([P, HALF], U8, name="vs_lo", align_bytes=64)
        nc.vector.tensor_copy(vs_lo[:], vs_pool[:].indirect(list_halves[0]))

        neg_max = sb.tile([P, 1], F32, name="neg_max", tag="keys_chain", align_bytes=64)
        nc.vector.tensor_reduce(out=neg_max[:], in_=a[:], axis=AX.X, op=ALU.max, negate=True)
        vs_hi = sb.tile([P, HALF], U8, name="vs_hi", tag="ks_then_vs", align_bytes=64)
        nc.vector.tensor_copy(vs_hi[:], vs_pool[:].indirect(list_halves[1]))
        g_codes = sb.tile([P, Q], U32, name="g_codes", tag="row_codes", align_bytes=64)
        g_scales = sb.tile([P, Q], U8, name="g_scales", align_bytes=64)
        nc.vector.quantize_mx(
            out=g_codes[:].bitcast(FP8X4), scales=g_scales[:], in_=g_bf[:].rearrange("p w j -> p (w j)")
        )
        p = sb.tile([P, I], F32, name="p", tag="g_then_p")
        s = sb.tile([P, G], F32, name="s")
        z_halves = sb.tile([P, 2], F32, name="z_halves")
        for h, (cols, groups) in enumerate(zip(halves, group_halves)):
            nc.scalar.activation(
                out=p[:, cols], in_=a[:, cols], func=ACT.Exp, bias=neg_max[:], scale=1.0, accum_out=z_halves[:, h : h + 1]
            )
            nc.vector.tensor_reduce(out=s[:, groups], in_=by_group(p[:, cols]), axis=AX.X, op=ALU.add)
        z_halves_share = sb.tile([P, 2], F32, name="z_halves_share")
        z_share = sb.tile([P, 1], F32, name="z_share")
        nc.scalar.activation(out=z_halves_share[:], in_=z_halves[:], func=ACT.Copy, scale=sh[:], accum_out=z_share[:])
        rest = sb.tile([P, 1], F32, name="rest")
        nc.gpsimd.tensor_scalar(
            out=rest[:], in0=sh[:], scalar1=-64.0, scalar2=64.0, op0=ALU.mult, op1=ALU.add
        )
        group_factor = sb.tile([P, 1], F32, name="group_factor")
        nc.gpsimd.tensor_scalar(
            out=group_factor[:], in0=sh[:], scalar1=32768.0, scalar2=-32768.0, op0=ALU.mult, op1=ALU.add
        )
        row_factor = sb.tile([P, 1], F32, name="row_factor")
        nc.gpsimd.tensor_scalar(
            out=row_factor[:], in0=sh[:], scalar1=-512.0, scalar2=0.0, op0=ALU.mult, op1=ALU.add
        )
        den = sb.tile([P, G], F32, name="den")
        nc.scalar.activation(out=den[:], in_=s[:], func=ACT.Identity, scale=rest[:], bias=z_share[:])

        vw = sb.tile([P, I], U32, name="vw", tag="keys_chain", align_bytes=64)
        c0 = [ps.tile([P, HALF], F32, name="c0_%d" % h) for h in range(2)]
        for cols, entries, vs, bank in zip(halves, list_halves, (vs_lo, vs_hi), c0):
            nc.vector.tensor_copy(vw[:, cols], vw_pool[:].indirect(entries))
            nc.tensor.matmul_mx(
                out=bank[:],
                lhsT=g_codes[:].bitcast(FP8X4),
                lhsT_scale=g_scales[:],
                rhs=vw[:, cols].bitcast(FP8X4),
                rhs_scale=vs[VAL_ROW:P, :],
                start=True,
                stop=True,
            )

        v1 = sb.tile([P, G], F32, name="v1")
        nc.vector.reciprocal(out=v1[:], in_=den[:])
        v1_sq = sb.tile([P, G], F32, name="v1_sq")
        nc.scalar.activation(out=v1_sq[:], in_=v1[:], func=ACT.Square)
        dvr = sb.tile([P, I], F32, name="dvr")
        dv1 = sb.tile([P, G], F32, name="dv1")
        for cols, bank in zip(halves, c0):
            nc.vector.tensor_tensor(out=dvr[:, cols], in0=bank[:], in1=p[:, cols], op=ALU.mult)
        for cols, groups in zip(halves, group_halves):
            nc.vector.tensor_reduce(out=dv1[:, groups], in_=by_group(dvr[:, cols]), axis=AX.X, op=ALU.add)
        row_terms = sb.tile([P, G], F32, name="row_terms")
        dz = sb.tile([P, 1], F32, name="dz")
        nc.vector.scalar_tensor_tensor(
            out=row_terms[:], in0=dv1[:], scalar=row_factor[:], in1=v1_sq[:], op0=ALU.mult, op1=ALU.mult, accum_out=dz[:]
        )
        ds = sb.tile([P, G], F32, name="ds")
        nc.vector.scalar_tensor_tensor(
            out=ds[:], in0=dv1[:], scalar=group_factor[:], in1=v1_sq[:], op0=ALU.mult, op1=ALU.mult
        )
        through_sums = sb.tile([P, I], F32, name="through_sums")
        nc.vector.scalar_tensor_tensor(
            out=by_group(through_sums[:]), in0=spread(ds[:]), scalar=dz[:], in1=by_group(p[:]), op0=ALU.add, op1=ALU.mult
        )
        direct = sb.tile([P, I], F32, name="direct")
        for cols, groups in zip(halves, group_halves):
            nc.vector.scalar_tensor_tensor(
                out=by_group(direct[:, cols]),
                in0=by_group(dvr[:, cols]),
                scalar=512.0,
                in1=spread(v1[:, groups]),
                op0=ALU.mult,
                op1=ALU.mult,
            )
        nc.vector.tensor_tensor(placed[:].indirect(offsets[:]), direct[:], through_sums[:], ALU.add)

        col = 0
        for n, width in enumerate(OUT_CHUNKS):
            cols = slice(col, col + width)
            total = sb.tile([P, width], F32, name="total%d" % n)
            nc.vector.tensor_tensor(out=total[:], in0=prior[:, cols], in1=placed[:, cols], op=ALU.add)
            nc.sync.dma_start(out=out[:, cols], in_=total[:])
            col += width
